import numpy as np
import ml_dtypes

BF16 = ml_dtypes.bfloat16


def bf(x):
    return np.asarray(x, np.float32).astype(BF16)


def f32(x):
    return np.asarray(x, np.float32)


def f64(x):
    return np.asarray(x).astype(np.float64)


def striped(idx):
    return np.tile(idx.reshape(-1, 16).T, (8, 1))


S, K, M, N, B, Q = 256, 128, 256, 256, 2, 128


def setup_inputs():
    return {"base": bf(np.random.standard_normal((B, M, S))), "x": bf(np.random.standard_normal((K, N))), "w": bf(np.random.standard_normal((K, M)) / np.sqrt(K)), "b": f32(0.5 * np.random.standard_normal((M, 1))), "offs": striped(np.random.permutation(S))}


def reference(base, x, w, b, offs):
    idx = offs[:16].T.reshape(-1)
    z = f64(base).copy()
    for i in range(B):
        z[i][:, idx[i * Q : (i + 1) * Q]] = f64(w).T @ f64(x)[:, i * Q : (i + 1) * Q]
    return z + f64(b)

@@ -1,0 +1,74 @@
+import concourse.mybir as mybir
+from concourse.masks import make_identity
+
+P = 128
+SEQS = 2
+BLOCKS = 2
+TOKENS = 256
+PIECE = 128
+PIECE_COLS = PIECE // 16
+
+FLOPS = 2 * P * (BLOCKS * P) * (SEQS * PIECE)
+
+BF16 = mybir.dt.bfloat16
+F32 = mybir.dt.float32
+U16 = mybir.dt.uint16
+
+
+def tile_scatter_matmul_kernel(tc, base, x, w, b, offs, out):
+    nc = tc.nc
+    windows_of = [(i, a) for i in range(SEQS) for a in range(BLOCKS)]
+
+    with (
+        tc.tile_pool(name="held", bufs=1) as held,
+        tc.psum_pool(name="psum", bufs=1) as psum,
+    ):
+        base_tiles = {}
+        for n, (i, a) in enumerate(windows_of):
+            base_tiles[(i, a)] = held.tile([P, TOKENS], BF16, name=f"base{i}{a}")
+            queue = nc.sync if n % 2 == 0 else nc.scalar
+            queue.dma_start(base_tiles[(i, a)][:], base[i, a * P : (a + 1) * P, :])
+
+        offsets = held.tile([P, SEQS * PIECE_COLS], U16, name="offsets")
+        nc.sync.dma_start(offsets[:], offs)
+        x_tile = held.tile([P, SEQS * PIECE], BF16, name="x_tile")
+        nc.sync.dma_start(x_tile[:], x)
+        w_tile = held.tile([P, BLOCKS * P], BF16, name="w_tile")
+        nc.scalar.dma_start(w_tile[:], w)
+        bias = held.tile([P, BLOCKS], F32, name="bias")
+        with nc.allow_non_contiguous_dma(reason="256 single float32 values, one to a partition"):
+            nc.scalar.dma_start(bias[:], b.rearrange("(a p) o -> p (a o)", p=P))
+
+        ident = held.tile([P, P], BF16, name="ident")
+        make_identity(nc, ident[:])
+
+        windows = {}
+        for i, a in windows_of:
+            windows[(i, a)] = psum.tile([P, TOKENS], F32, name=f"window{i}{a}")
+            nc.tensor.matmul(
+                windows[(i, a)][:], ident[:], base_tiles[(i, a)][:], start=True, stop=True
+            )
+
+        for i, a in windows_of:
+            piece = offsets[:, i * PIECE_COLS : (i + 1) * PIECE_COLS]
+            nc.tensor.matmul(
+                windows[(i, a)][:].indirect(piece),
+                w_tile[:, a * P : (a + 1) * P],
+                x_tile[:, i * PIECE : (i + 1) * PIECE],
+                start=True,
+                stop=True,
+            )
+
+        for n, (i, a) in enumerate(windows_of):
+            result = held.tile([P, TOKENS], F32, name=f"result{i}{a}")
+            if n % 2 == 0:
+                nc.vector.tensor_scalar_add(result[:], windows[(i, a)][:], bias[:, a : a + 1])
+                nc.sync.dma_start(out[i, a * P : (a + 1) * P, :], result[:])
+            else:
+                nc.scalar.activation(
+                    result[:],
+                    windows[(i, a)][:],
+                    mybir.ActivationFunctionType.Identity,
+                    bias=bias[:, a : a + 1],
+                )
+                nc.scalar.dma_start(out[i, a * P : (a + 1) * P, :], result[:])

@@ -8,6 +8,9 @@ TOKENS = 256
 PIECE = 128
 PIECE_COLS = PIECE // 16
 
+WARM_COLS = 512
+WARM_MATMULS = 3
+
 FLOPS = 2 * P * (BLOCKS * P) * (SEQS * PIECE)
 
 BF16 = mybir.dt.bfloat16
@@ -41,6 +44,12 @@ def tile_scatter_matmul_kernel(tc, base, x, w, b, offs, out):
 
         ident = held.tile([P, P], BF16, name="ident")
         make_identity(nc, ident[:])
+
+        zeros = held.tile([P, WARM_COLS], BF16, name="zeros")
+        nc.vector.memset(zeros[:], 0.0)
+        warm_bank = psum.tile([P, WARM_COLS], F32, name="warm_bank")
+        for n in range(WARM_MATMULS):
+            nc.tensor.matmul(warm_bank[:], zeros[:, 0:P], zeros[:], start=True, stop=True)
 
         windows = {}
         for i, a in windows_of:

@@ -47,6 +47,8 @@ def tile_scatter_matmul_kernel(tc, base, x, w, b, offs, out):
 
         zeros = held.tile([P, WARM_COLS], BF16, name="zeros")
         nc.vector.memset(zeros[:], 0.0)
+        warm_act = held.tile([P, 1], F32, name="warm_act")
+        nc.scalar.activation(warm_act[:], zeros[:, 0:1], mybir.ActivationFunctionType.Identity)
         warm_bank = psum.tile([P, WARM_COLS], F32, name="warm_bank")
         for n in range(WARM_MATMULS):
             nc.tensor.matmul(warm_bank[:], zeros[:, 0:P], zeros[:], start=True, stop=True)

@@ -8,9 +8,6 @@ TOKENS = 256
 PIECE = 128
 PIECE_COLS = PIECE // 16
 
-WARM_COLS = 512
-WARM_MATMULS = 3
-
 FLOPS = 2 * P * (BLOCKS * P) * (SEQS * PIECE)
 
 BF16 = mybir.dt.bfloat16
@@ -45,13 +42,10 @@ def tile_scatter_matmul_kernel(tc, base, x, w, b, offs, out):
         ident = held.tile([P, P], BF16, name="ident")
         make_identity(nc, ident[:])
 
-        zeros = held.tile([P, WARM_COLS], BF16, name="zeros")
-        nc.vector.memset(zeros[:], 0.0)
+        zero = held.tile([P, 1], F32, name="zero")
+        nc.vector.memset(zero[:], 0.0)
         warm_act = held.tile([P, 1], F32, name="warm_act")
-        nc.scalar.activation(warm_act[:], zeros[:, 0:1], mybir.ActivationFunctionType.Identity)
-        warm_bank = psum.tile([P, WARM_COLS], F32, name="warm_bank")
-        for n in range(WARM_MATMULS):
-            nc.tensor.matmul(warm_bank[:], zeros[:, 0:P], zeros[:], start=True, stop=True)
+        nc.scalar.activation(warm_act[:], zero[:], mybir.ActivationFunctionType.Identity)
 
         windows = {}
         for i, a in windows_of:

@@ -8,6 +8,9 @@ TOKENS = 256
 PIECE = 128
 PIECE_COLS = PIECE // 16
 
+WARM_COLS = 512
+WARM_MATMULS = 3
+
 FLOPS = 2 * P * (BLOCKS * P) * (SEQS * PIECE)
 
 BF16 = mybir.dt.bfloat16
@@ -23,6 +26,18 @@ def tile_scatter_matmul_kernel(tc, base, x, w, b, offs, out):
         tc.tile_pool(name="held", bufs=1) as held,
         tc.psum_pool(name="psum", bufs=1) as psum,
     ):
+        zero_bf = held.tile([P, 1], BF16, name="zero_bf")
+        nc.gpsimd.memset(zero_bf[:], 0.0)
+        warm_bank = psum.tile([P, WARM_COLS], F32, name="warm_bank")
+        for n in range(WARM_MATMULS):
+            nc.tensor.matmul(
+                warm_bank[:],
+                zero_bf[:].to_broadcast([P, P]),
+                zero_bf[:].to_broadcast([P, WARM_COLS]),
+                start=True,
+                stop=True,
+            )
+
         base_tiles = {}
         for n, (i, a) in enumerate(windows_of):
             base_tiles[(i, a)] = held.tile([P, TOKENS], BF16, name=f"base{i}{a}")

@@ -38,11 +38,11 @@ def tile_scatter_matmul_kernel(tc, base, x, w, b, offs, out):
                 stop=True,
             )
 
-        base_tiles = {}
-        for n, (i, a) in enumerate(windows_of):
-            base_tiles[(i, a)] = held.tile([P, TOKENS], BF16, name=f"base{i}{a}")
-            queue = nc.sync if n % 2 == 0 else nc.scalar
-            queue.dma_start(base_tiles[(i, a)][:], base[i, a * P : (a + 1) * P, :])
+        base_tiles = []
+        for i in range(SEQS):
+            base_tiles.append(held.tile([P, BLOCKS * TOKENS], BF16, name=f"base{i}"))
+            queue = nc.sync if i % 2 == 0 else nc.scalar
+            queue.dma_start(base_tiles[i][:], base[i].rearrange("(p a) t -> p (a t)", a=BLOCKS))
 
         offsets = held.tile([P, SEQS * PIECE_COLS], U16, name="offsets")
         nc.sync.dma_start(offsets[:], offs)
@@ -51,8 +51,7 @@ def tile_scatter_matmul_kernel(tc, base, x, w, b, offs, out):
         w_tile = held.tile([P, BLOCKS * P], BF16, name="w_tile")
         nc.scalar.dma_start(w_tile[:], w)
         bias = held.tile([P, BLOCKS], F32, name="bias")
-        with nc.allow_non_contiguous_dma(reason="256 single float32 values, one to a partition"):
-            nc.scalar.dma_start(bias[:], b.rearrange("(a p) o -> p (a o)", p=P))
+        nc.scalar.dma_start(bias[:], b.rearrange("(p a) o -> p (a o)", a=BLOCKS))
 
         ident = held.tile([P, P], BF16, name="ident")
         make_identity(nc, ident[:])
@@ -66,29 +65,31 @@ def tile_scatter_matmul_kernel(tc, base, x, w, b, offs, out):
         for i, a in windows_of:
             windows[(i, a)] = psum.tile([P, TOKENS], F32, name=f"window{i}{a}")
             nc.tensor.matmul(
-                windows[(i, a)][:], ident[:], base_tiles[(i, a)][:], start=True, stop=True
+                windows[(i, a)][:],
+                ident[:],
+                base_tiles[i][:, a * TOKENS : (a + 1) * TOKENS],
+                start=True,
+                stop=True,
             )
 
         for i, a in windows_of:
             piece = offsets[:, i * PIECE_COLS : (i + 1) * PIECE_COLS]
             nc.tensor.matmul(
                 windows[(i, a)][:].indirect(piece),
-                w_tile[:, a * P : (a + 1) * P],
+                w_tile[:, a::BLOCKS],
                 x_tile[:, i * PIECE : (i + 1) * PIECE],
                 start=True,
                 stop=True,
             )
 
-        for n, (i, a) in enumerate(windows_of):
-            result = held.tile([P, TOKENS], F32, name=f"result{i}{a}")
-            if n % 2 == 0:
-                nc.vector.tensor_scalar_add(result[:], windows[(i, a)][:], bias[:, a : a + 1])
-                nc.sync.dma_start(out[i, a * P : (a + 1) * P, :], result[:])
-            else:
-                nc.scalar.activation(
-                    result[:],
-                    windows[(i, a)][:],
-                    mybir.ActivationFunctionType.Identity,
-                    bias=bias[:, a : a + 1],
-                )
-                nc.scalar.dma_start(out[i, a * P : (a + 1) * P, :], result[:])
+        for i in range(SEQS):
+            result = held.tile([P, BLOCKS * TOKENS], F32, name=f"result{i}")
+            nc.vector.tensor_scalar_add(result[:, :TOKENS], windows[(i, 0)][:], bias[:, 0:1])
+            nc.scalar.activation(
+                result[:, TOKENS:],
+                windows[(i, 1)][:],
+                mybir.ActivationFunctionType.Identity,
+                bias=bias[:, 1:2],
+            )
+            queue = nc.sync if i % 2 == 0 else nc.scalar
+            queue.dma_start(out[i].rearrange("(p a) t -> p (a t)", a=BLOCKS), result[:])

@@ -91,5 +91,4 @@ def tile_scatter_matmul_kernel(tc, base, x, w, b, offs, out):
                 mybir.ActivationFunctionType.Identity,
                 bias=bias[:, 1:2],
             )
-            queue = nc.sync if i % 2 == 0 else nc.scalar
-            queue.dma_start(out[i].rearrange("(p a) t -> p (a t)", a=BLOCKS), result[:])
+            nc.sync.dma_start(out[i].rearrange("(p a) t -> p (a t)", a=BLOCKS), result[:])

import concourse.mybir as mybir
from concourse.masks import make_identity

P = 128
SEQS = 2
BLOCKS = 2
TOKENS = 256
PIECE = 128
PIECE_COLS = PIECE // 16

WARM_COLS = 512
WARM_MATMULS = 3

FLOPS = 2 * P * (BLOCKS * P) * (SEQS * PIECE)

BF16 = mybir.dt.bfloat16
F32 = mybir.dt.float32
U16 = mybir.dt.uint16


def tile_scatter_matmul_kernel(tc, base, x, w, b, offs, out):
    nc = tc.nc
    windows_of = [(i, a) for i in range(SEQS) for a in range(BLOCKS)]

    with (
        tc.tile_pool(name="held", bufs=1) as held,
        tc.psum_pool(name="psum", bufs=1) as psum,
    ):
        zero_bf = held.tile([P, 1], BF16, name="zero_bf")
        nc.gpsimd.memset(zero_bf[:], 0.0)
        warm_bank = psum.tile([P, WARM_COLS], F32, name="warm_bank")
        for n in range(WARM_MATMULS):
            nc.tensor.matmul(
                warm_bank[:],
                zero_bf[:].to_broadcast([P, P]),
                zero_bf[:].to_broadcast([P, WARM_COLS]),
                start=True,
                stop=True,
            )

        base_tiles = []
        for i in range(SEQS):
            base_tiles.append(held.tile([P, BLOCKS * TOKENS], BF16, name=f"base{i}"))
            queue = nc.sync if i % 2 == 0 else nc.scalar
            queue.dma_start(base_tiles[i][:], base[i].rearrange("(p a) t -> p (a t)", a=BLOCKS))

        offsets = held.tile([P, SEQS * PIECE_COLS], U16, name="offsets")
        nc.sync.dma_start(offsets[:], offs)
        x_tile = held.tile([P, SEQS * PIECE], BF16, name="x_tile")
        nc.sync.dma_start(x_tile[:], x)
        w_tile = held.tile([P, BLOCKS * P], BF16, name="w_tile")
        nc.scalar.dma_start(w_tile[:], w)
        bias = held.tile([P, BLOCKS], F32, name="bias")
        nc.scalar.dma_start(bias[:], b.rearrange("(p a) o -> p (a o)", a=BLOCKS))

        ident = held.tile([P, P], BF16, name="ident")
        make_identity(nc, ident[:])

        zero = held.tile([P, 1], F32, name="zero")
        nc.vector.memset(zero[:], 0.0)
        warm_act = held.tile([P, 1], F32, name="warm_act")
        nc.scalar.activation(warm_act[:], zero[:], mybir.ActivationFunctionType.Identity)

        windows = {}
        for i, a in windows_of:
            windows[(i, a)] = psum.tile([P, TOKENS], F32, name=f"window{i}{a}")
            nc.tensor.matmul(
                windows[(i, a)][:],
                ident[:],
                base_tiles[i][:, a * TOKENS : (a + 1) * TOKENS],
                start=True,
                stop=True,
            )

        for i, a in windows_of:
            piece = offsets[:, i * PIECE_COLS : (i + 1) * PIECE_COLS]
            nc.tensor.matmul(
                windows[(i, a)][:].indirect(piece),
                w_tile[:, a::BLOCKS],
                x_tile[:, i * PIECE : (i + 1) * PIECE],
                start=True,
                stop=True,
            )

        for i in range(SEQS):
            result = held.tile([P, BLOCKS * TOKENS], F32, name=f"result{i}")
            nc.vector.tensor_scalar_add(result[:, :TOKENS], windows[(i, 0)][:], bias[:, 0:1])
            nc.scalar.activation(
                result[:, TOKENS:],
                windows[(i, 1)][:],
                mybir.ActivationFunctionType.Identity,
                bias=bias[:, 1:2],
            )
            nc.sync.dma_start(out[i].rearrange("(p a) t -> p (a t)", a=BLOCKS), result[:])
